import numpy as np
import ml_dtypes


def mxq(x, axis, fmt="e4m3"):
    dtype, down = {"e4m3": (ml_dtypes.float8_e4m3fn, 7), "e5m2": (ml_dtypes.float8_e5m2, 14)}[fmt]
    v = np.moveaxis(np.asarray(x, np.float32).astype(ml_dtypes.bfloat16).astype(np.float64), axis, -1)
    blocks = v.reshape(v.shape[:-1] + (-1, 32))
    amax = np.abs(blocks).max(-1, keepdims=True)
    byte = np.maximum(np.where(amax > 0, np.frexp(amax)[1] - 1 + 127, 0) - down, 1)
    scale = np.exp2(byte - 127.0)
    codes = (blocks / scale).astype(np.float32).astype(dtype).astype(np.float64)
    return np.moveaxis((codes * scale).reshape(v.shape), -1, axis)


WIDE = False


def mx_kscale(k):
    if not WIDE:
        return np.ones(k)
    levels = np.array([10, -10, 5, -5, 0])
    if k % 512:
        return np.exp2(np.random.permutation(np.resize(levels, k // 32))).repeat(32)
    a = np.empty((k // 512, 16))
    for p in range(k // 512):
        a[p, :8] = np.random.permutation(np.resize(levels, 8))
        for g in range(8):
            far = levels[np.abs(levels - a[p, g]) >= 10]
            a[p, g + 8] = far[np.random.randint(len(far))]
    return np.exp2(a.ravel()).repeat(32)


def f64(x):
    return np.asarray(x).astype(np.float64)


def striped(idx):
    return np.tile(np.asarray(idx).reshape(-1, 16).T, (8, 1)).astype(np.uint16)


def unstriped(offs):
    return offs[:16].T.reshape(-1).astype(np.int64)


E2M1 = np.array([0.0, 0.5, 1.0, 1.5, 2.0, 3.0, 4.0, 6.0, -0.0, -0.5, -1.0, -1.5, -2.0, -3.0, -4.0, -6.0])


def pack_weight(w, fmt):
    k, n = w.shape
    w = f64(np.asarray(w, np.float32).astype(ml_dtypes.bfloat16)).reshape(k // 32, 32, n)
    amax = np.abs(w).max(1)
    if fmt == "e4m3":
        byte = np.frexp(amax)[1] - 1 + 127 - 7
    else:
        mant, ex = np.frexp(amax / 6.0)
        byte = np.where(mant > 0.5, ex, ex - 1) + 127
    byte = np.clip(np.where(amax > 0, byte, 1), 1, 254)
    scaled = (w * np.exp2(127.0 - byte)[:, None, :]).reshape(k, n).astype(np.float32)
    by_word = np.ascontiguousarray(scaled.reshape(k // 512, 128, 4, n).transpose(0, 1, 3, 2))
    if fmt == "e4m3":
        words = by_word.astype(ml_dtypes.float8_e4m3fn).view(np.uint8)
    else:
        c = by_word.astype(ml_dtypes.float4_e2m1fn).view(np.uint8) & 0xF
        words = (c[..., 0::2] | (c[..., 1::2] << 4)).reshape(k // 512, 128, 2 * n)
    return np.ascontiguousarray(words), np.ascontiguousarray(byte.astype(np.uint8).reshape(k // 512, 16, n))


def unpack_weight(words, scales, fmt):
    g, _, n = scales.shape
    words = np.ascontiguousarray(words).reshape(g, 128, n, -1)
    if fmt == "e4m3":
        vals = words.view(ml_dtypes.float8_e4m3fn).astype(np.float64)
    else:
        nib = np.empty((g, 128, n, 4), np.uint8)
        nib[..., 0::2] = words & 0xF
        nib[..., 1::2] = words >> 4
        vals = E2M1[nib]
    vals = vals * np.repeat(np.exp2(scales.astype(np.float64) - 127.0), 8, axis=1)[..., None]
    return vals.transpose(0, 1, 3, 2).reshape(g * 512, n)


def bf(x):
    return np.asarray(x, np.float32).astype(ml_dtypes.bfloat16)


def planes(Y):
    r, m = Y.shape
    b = f64(bf(Y)).reshape(r // 32, 32, m)
    amax = np.abs(b).max(1)
    byte = np.clip(np.where(amax > 0, np.frexp(amax)[1] - 1 + 127 - 7, 1), 1, 254)
    codes = (b * np.exp2(127.0 - byte)[:, None, :]).reshape(r, m).astype(np.float32).astype(ml_dtypes.float8_e4m3fn).view(np.uint8)
    words = codes.reshape(r // 512, 128, 4, m).transpose(0, 1, 3, 2)
    return np.ascontiguousarray(words), np.ascontiguousarray(byte.astype(np.uint8).reshape(r // 512, 16, m))


K, T, S, J, I = 1024, 1024, 1024, 512, 512


def setup_inputs():
    n = np.random.standard_normal
    idx = np.random.permutation(T)[:J]
    idx2 = np.random.permutation(S)[:I]
    fk = mx_kscale(K)
    xbp = pack_weight(n((K, S)) / fk[:, None], "e2m1")
    return {
        "xa": (n((K, T)) * 0.1 * fk[:, None]).astype(np.float32),
        "xb_words": xbp[0],
        "xb_scales": xbp[1],
        "cw1": (np.random.uniform(16.0, 64.0, (1, I))).astype(np.float32),
        "offs": striped(idx),
        "offs2": striped(idx2),
    }


def reference(xa, xb_words, xb_scales, cw1, offs, offs2):
    idx = unstriped(offs)
    idx2 = unstriped(offs2)
    xbu = unpack_weight(xb_words, xb_scales, "e2m1")
    xaidxq = mxq(f64(xa)[:, idx], 0, "e4m3")
    xbidx2g = xbu[:, idx2]
    a = xaidxq.T @ xbidx2g
    r = np.maximum(a, 0.0)
    y = r * f64(cw1) / (np.sum(r, axis=1, keepdims=True) + 1.0)
    words, scales = planes(y)
    return y, words, scales

@@ -1,0 +1,166 @@
+from contextlib import ExitStack
+
+import concourse.mybir as mybir
+from concourse.masks import make_identity
+
+K, T, S, J, I = 1024, 1024, 1024, 512, 512
+FLOPS = 2 * K * J * I
+
+F32 = mybir.dt.float32
+BF16 = mybir.dt.bfloat16
+I32 = mybir.dt.int32
+U32 = mybir.dt.uint32
+U16 = mybir.dt.uint16
+U8 = mybir.dt.uint8
+FP8X4 = mybir.dt.float8_e4m3fn_x4
+FP4X4 = mybir.dt.float4_e2m1fn_x4
+ACT = mybir.ActivationFunctionType
+ALU = mybir.AluOpType
+
+P = 128
+PACK = 4
+K_PASS = P * PACK
+PASSES = K // K_PASS
+CHUNK = 512
+LAST_SCALAR_COLS = 160
+OUT_SCALAR_COLS = 160
+
+
+def tile_list_affinity_of_two_lists_pl_kernel(tc, xa, xb_words, xb_scales, cw1, offs, offs2, out_0, out_1, out_2):
+    nc = tc.nc
+    with ExitStack() as ctx:
+        keep = ctx.enter_context(tc.tile_pool(name="keep", bufs=1))
+        psum = ctx.enter_context(tc.psum_pool(name="psum", bufs=1))
+
+        b_scales = keep.tile([P, S], U8, name="b_scales")
+        nc.vector.memset(b_scales[:].bitcast(I32), 0)
+        for q in range(4):
+            nc.scalar.dma_start(
+                b_scales[32 * q : 32 * q + 8, :].bitcast(I32),
+                xb_scales[:, 4 * q : 4 * q + 4, :].bitcast(I32),
+            )
+        list_b = keep.tile([P, I // 16], U16, name="list_b")
+        list_a = keep.tile([P, J // 16], U16, name="list_a")
+        nc.sync.dma_start(list_b[:], offs2)
+        b_words = []
+        for a in range(PASSES):
+            words = keep.tile([P, S], U16, name="b_words%d" % a)
+            nc.sync.dma_start(words[:].bitcast(I32), xb_words[a].bitcast(I32))
+            b_words.append(words)
+        nc.sync.dma_start(list_a[:], offs)
+
+        raw = {}
+        for a in range(PASSES):
+            rows = xa[a * K_PASS : (a + 1) * K_PASS, :].rearrange("(p u e) c -> u p e c", u=2, e=2)
+            for u in range(2):
+                for h in range(T // CHUNK):
+                    chunk = keep.tile([P, 2, CHUNK], F32, name="raw%d%d%d" % (a, u, h))
+                    nc.sync.dma_start(chunk[:], rows[u][:, :, h * CHUNK : (h + 1) * CHUNK])
+                    raw[a, u, h] = chunk
+
+        cw_col = keep.tile([P, PACK], F32, name="cw_col")
+        nc.gpsimd.dma_start(cw_col[:], cw1.rearrange("o (n m) -> (o n) m", m=PACK))
+        moved_scales = keep.tile([P, I], U8, name="moved_scales", align_bytes=64)
+        nc.vector.memset(moved_scales[:].bitcast(I32), 0)
+        ident = keep.tile([P, P], F32, name="ident")
+        make_identity(nc, ident[:])
+
+        cw_all = psum.tile([P, PACK, P], F32, name="cw_all")
+        for m in range(PACK):
+            nc.tensor.transpose(cw_all[:, m, :], cw_col[:, m : m + 1].to_broadcast([P, P]), ident[:])
+
+        picked_words = []
+        for a in range(PASSES):
+            picked = keep.tile([P, I], U16, name="picked_words%d" % a, align_bytes=64)
+            nc.vector.tensor_copy(picked[:], b_words[a][:].indirect(list_b[:]))
+            picked_words.append(picked)
+        picked_scales = keep.tile([P, I], U8, name="picked_scales", align_bytes=64)
+        nc.vector.tensor_copy(picked_scales[:], b_scales[:].indirect(list_b[:]))
+        for q in range(4):
+            nc.sync.dma_start(
+                moved_scales[32 * q : 32 * q + 4, :].bitcast(I32),
+                picked_scales[32 * q + 4 : 32 * q + 8, :].bitcast(I32),
+            )
+        b_planes = [picked_scales, moved_scales]
+
+        acc = [psum.tile([P, I], F32, name="acc%d" % t) for t in range(PACK)]
+
+        for a in range(PASSES):
+            last_pass = a == PASSES - 1
+            picked_a = keep.tile([P, 2, J], F32, name="picked_a%d" % a)
+            for u in range(2):
+                pairs = keep.tile([P, T], F32, name="pairs%d%d" % (a, u))
+                pairs_bf = pairs[:].bitcast(BF16).rearrange("p (c e) -> p c e", e=2)
+                for h in range(T // CHUNK):
+                    src = raw[a, u, h][:].rearrange("p e c -> p c e")
+                    c0 = h * CHUNK
+                    cut = LAST_SCALAR_COLS if (last_pass and u == 1 and h == T // CHUNK - 1) else CHUNK
+                    nc.scalar.activation(pairs_bf[:, c0 : c0 + cut, :], src[:, 0:cut, :], ACT.Copy)
+                    if cut < CHUNK:
+                        nc.vector.tensor_copy(pairs_bf[:, c0 + cut : c0 + CHUNK, :], src[:, cut:CHUNK, :])
+                nc.vector.tensor_copy(picked_a[:, u, :], pairs[:].indirect(list_a[:]))
+            dealt_src = picked_a[:].rearrange("p u (mp mi t) -> p mp t mi u", mi=2, t=PACK)
+            dealt = []
+            for half in range(2):
+                tile = keep.tile([P, 2 * P * 2], F32, name="dealt%d%d" % (a, half), align_bytes=64)
+                dst = tile[:].rearrange("p (t mp mi u) -> p mp t mi u", t=2, mi=2, u=2)
+                src = dealt_src[:, :, 2 * half : 2 * half + 2, :, :]
+                if last_pass and half == 1:
+                    nc.scalar.copy(dst, src)
+                else:
+                    nc.vector.tensor_copy(dst, src)
+                dealt.append(tile)
+            for half in range(2):
+                codes = keep.tile([P, 2 * P], U32, name="a_codes%d%d" % (a, half), align_bytes=64)
+                scales = keep.tile([P, 2 * P], U8, name="a_scales%d%d" % (a, half), align_bytes=64)
+                nc.vector.quantize_mx(out=codes[:].bitcast(FP8X4), scales=scales[:], in_=dealt[half][:].bitcast(BF16))
+                for tt in range(2):
+                    cols = slice(tt * P, (tt + 1) * P)
+                    nc.tensor.matmul_mx(
+                        out=acc[2 * half + tt][:],
+                        lhsT=codes[:, cols].bitcast(FP8X4),
+                        lhsT_scale=scales[:, cols],
+                        rhs=picked_words[a][:].bitcast(FP4X4),
+                        rhs_scale=b_planes[a][:],
+                        start=(a == 0),
+                        stop=last_pass,
+                    )
+
+        y = keep.tile([P, PACK, I], F32, name="y")
+        out_rows = out_0.rearrange("(p t) i -> t p i", t=PACK)
+        cw_cols = cw_all[:].rearrange("p m n -> p n m")
+        for t in range(PACK):
+            relu = keep.tile([P, I], F32, name="relu%d" % t)
+            total = keep.tile([P, 1], F32, name="total%d" % t)
+            denom = keep.tile([P, 1], F32, name="denom%d" % t)
+            inv = keep.tile([P, 1], F32, name="inv%d" % t)
+            nc.scalar.activation(relu[:], acc[t][:], ACT.Relu, accum_out=total[:])
+            nc.vector.tensor_scalar_add(denom[:], total[:], 1.0)
+            nc.vector.reciprocal(inv[:], denom[:])
+            nc.vector.scalar_tensor_tensor(
+                y[:, t, :].rearrange("p (n m) -> p n m", m=PACK),
+                relu[:].rearrange("p (n m) -> p n m", m=PACK),
+                inv[:],
+                cw_cols,
+                ALU.mult,
+                ALU.mult,
+            )
+            nc.sync.dma_start(out_rows[t], y[:, t, :])
+
+        y_bf = keep.tile([P, I, PACK], BF16, name="y_bf", align_bytes=64)
+        y_src = y[:].rearrange("p t (c i) -> p c t i", i=4)
+        y_dst = y_bf[:].rearrange("p (c i) t -> p c t i", i=4)
+        cut = OUT_SCALAR_COLS // 4
+        nc.scalar.copy(y_dst[:, 0:cut], y_src[:, 0:cut])
+        nc.vector.tensor_copy(y_dst[:, cut:], y_src[:, cut:])
+        y_codes = keep.tile([P, I], U32, name="y_codes", align_bytes=64)
+        y_scales = keep.tile([P, I], U8, name="y_scales", align_bytes=64)
+        nc.vector.quantize_mx(
+            out=y_codes[:].bitcast(FP8X4), scales=y_scales[:], in_=y_bf[:].rearrange("p c t -> p (c t)")
+        )
+        nc.sync.dma_start(out_1[0].rearrange("p c r -> p (c r)").bitcast(I32), y_codes[:].bitcast(I32))
+        for q in range(4):
+            queue = nc.scalar if q % 2 else nc.sync
+            queue.dma_start(
+                out_2[0, 4 * q : 4 * q + 4, :].bitcast(I32), y_scales[32 * q : 32 * q + 4, :].bitcast(I32)
+            )

@@ -20,73 +20,83 @@ ALU = mybir.AluOpType
 P = 128
 PACK = 4
 K_PASS = P * PACK
-PASSES = K // K_PASS
+PASS_ORDER = (0, 1)
 CHUNK = 512
+HALF = I // 2
 LAST_SCALAR_COLS = 160
-OUT_SCALAR_COLS = 160
+OUT_SCALAR_COLS = 192
 
 
 def tile_list_affinity_of_two_lists_pl_kernel(tc, xa, xb_words, xb_scales, cw1, offs, offs2, out_0, out_1, out_2):
     nc = tc.nc
+    first, last = PASS_ORDER
     with ExitStack() as ctx:
         keep = ctx.enter_context(tc.tile_pool(name="keep", bufs=1))
         psum = ctx.enter_context(tc.psum_pool(name="psum", bufs=1))
 
         b_scales = keep.tile([P, S], U8, name="b_scales")
-        nc.vector.memset(b_scales[:].bitcast(I32), 0)
-        for q in range(4):
-            nc.scalar.dma_start(
-                b_scales[32 * q : 32 * q + 8, :].bitcast(I32),
-                xb_scales[:, 4 * q : 4 * q + 4, :].bitcast(I32),
-            )
+        nc.gpsimd.memset(b_scales[32:64, :].bitcast(I32), 0)
+        nc.gpsimd.memset(b_scales[64:P, :].bitcast(I32), 0)
+        cw_col = keep.tile([P, PACK], F32, name="cw_col")
+        nc.gpsimd.dma_start(cw_col[:], cw1.rearrange("o (n m) -> (o n) m", m=PACK))
+        b_planes = keep.tile([P, 2 * I], U8, name="b_planes", align_bytes=64)
+        nc.gpsimd.memset(b_planes[:].bitcast(I32), 0)
+        ident = keep.tile([P, P], F32, name="ident")
+        make_identity(nc, ident[:])
+
+        raw = {}
+        b_words = {}
+
+        def load_words(a):
+            words = keep.tile([P, S], U16, name="b_words%d" % a)
+            nc.sync.dma_start(words[:].bitcast(I32), xb_words[a].bitcast(I32))
+            b_words[a] = words
+
+        def load_chunk(a, u, h):
+            rows = xa[a * K_PASS : (a + 1) * K_PASS, :].rearrange("(p u e) c -> u p e c", u=2, e=2)
+            chunk = keep.tile([P, 2, CHUNK], F32, name="raw%d%d%d" % (a, u, h))
+            nc.sync.dma_start(chunk[:], rows[u][:, :, h * CHUNK : (h + 1) * CHUNK])
+            raw[a, u, h] = chunk
+
+        chunks = [(a, u, h) for a in PASS_ORDER for u in range(2) for h in range(T // CHUNK)]
         list_b = keep.tile([P, I // 16], U16, name="list_b")
         list_a = keep.tile([P, J // 16], U16, name="list_a")
         nc.sync.dma_start(list_b[:], offs2)
-        b_words = []
-        for a in range(PASSES):
-            words = keep.tile([P, S], U16, name="b_words%d" % a)
-            nc.sync.dma_start(words[:].bitcast(I32), xb_words[a].bitcast(I32))
-            b_words.append(words)
+        load_words(first)
+        nc.sync.dma_start(b_scales[0:32, :].bitcast(I32), xb_scales.rearrange("z q c -> (z q) c").bitcast(I32))
+        for chunk in chunks[:2]:
+            load_chunk(*chunk)
+        load_words(last)
         nc.sync.dma_start(list_a[:], offs)
+        for chunk in chunks[2:]:
+            load_chunk(*chunk)
 
-        raw = {}
-        for a in range(PASSES):
-            rows = xa[a * K_PASS : (a + 1) * K_PASS, :].rearrange("(p u e) c -> u p e c", u=2, e=2)
-            for u in range(2):
-                for h in range(T // CHUNK):
-                    chunk = keep.tile([P, 2, CHUNK], F32, name="raw%d%d%d" % (a, u, h))
-                    nc.sync.dma_start(chunk[:], rows[u][:, :, h * CHUNK : (h + 1) * CHUNK])
-                    raw[a, u, h] = chunk
+        picked_words = {}
 
-        cw_col = keep.tile([P, PACK], F32, name="cw_col")
-        nc.gpsimd.dma_start(cw_col[:], cw1.rearrange("o (n m) -> (o n) m", m=PACK))
-        moved_scales = keep.tile([P, I], U8, name="moved_scales", align_bytes=64)
-        nc.vector.memset(moved_scales[:].bitcast(I32), 0)
-        ident = keep.tile([P, P], F32, name="ident")
-        make_identity(nc, ident[:])
+        def pick_words(a):
+            picked = keep.tile([P, I], U16, name="picked_words%d" % a, align_bytes=64)
+            nc.vector.tensor_copy(picked[:], b_words[a][:].indirect(list_b[:]))
+            picked_words[a] = picked
+
+        pick_words(first)
+        picked_scales = keep.tile([P, I], U8, name="picked_scales", align_bytes=64)
+        nc.vector.tensor_copy(picked_scales[:], b_scales[:].indirect(list_b[:]))
+        pick_words(last)
+        for a in PASS_ORDER:
+            queue = nc.gpsimd if a == first else nc.sync
+            for q in range(4):
+                queue.dma_start(
+                    b_planes[32 * q : 32 * q + 4, a * I : (a + 1) * I].bitcast(I32),
+                    picked_scales[16 * a + 4 * q : 16 * a + 4 * q + 4, :].bitcast(I32),
+                )
 
         cw_all = psum.tile([P, PACK, P], F32, name="cw_all")
         for m in range(PACK):
             nc.tensor.transpose(cw_all[:, m, :], cw_col[:, m : m + 1].to_broadcast([P, P]), ident[:])
 
-        picked_words = []
-        for a in range(PASSES):
-            picked = keep.tile([P, I], U16, name="picked_words%d" % a, align_bytes=64)
-            nc.vector.tensor_copy(picked[:], b_words[a][:].indirect(list_b[:]))
-            picked_words.append(picked)
-        picked_scales = keep.tile([P, I], U8, name="picked_scales", align_bytes=64)
-        nc.vector.tensor_copy(picked_scales[:], b_scales[:].indirect(list_b[:]))
-        for q in range(4):
-            nc.sync.dma_start(
-                moved_scales[32 * q : 32 * q + 4, :].bitcast(I32),
-                picked_scales[32 * q + 4 : 32 * q + 8, :].bitcast(I32),
-            )
-        b_planes = [picked_scales, moved_scales]
-
         acc = [psum.tile([P, I], F32, name="acc%d" % t) for t in range(PACK)]
 
-        for a in range(PASSES):
-            last_pass = a == PASSES - 1
+        for a in PASS_ORDER:
             picked_a = keep.tile([P, 2, J], F32, name="picked_a%d" % a)
             for u in range(2):
                 pairs = keep.tile([P, T], F32, name="pairs%d%d" % (a, u))
@@ -94,7 +104,8 @@ def tile_list_affinity_of_two_lists_pl_kernel(tc, xa, xb_words, xb_scales, cw1, 
                 for h in range(T // CHUNK):
                     src = raw[a, u, h][:].rearrange("p e c -> p c e")
                     c0 = h * CHUNK
-                    cut = LAST_SCALAR_COLS if (last_pass and u == 1 and h == T // CHUNK - 1) else CHUNK
+                    shared = h == T // CHUNK - 1 and u == 1
+                    cut = LAST_SCALAR_COLS if shared else CHUNK
                     nc.scalar.activation(pairs_bf[:, c0 : c0 + cut, :], src[:, 0:cut, :], ACT.Copy)
                     if cut < CHUNK:
                         nc.vector.tensor_copy(pairs_bf[:, c0 + cut : c0 + CHUNK, :], src[:, cut:CHUNK, :])
@@ -105,46 +116,60 @@ def tile_list_affinity_of_two_lists_pl_kernel(tc, xa, xb_words, xb_scales, cw1, 
                 tile = keep.tile([P, 2 * P * 2], F32, name="dealt%d%d" % (a, half), align_bytes=64)
                 dst = tile[:].rearrange("p (t mp mi u) -> p mp t mi u", t=2, mi=2, u=2)
                 src = dealt_src[:, :, 2 * half : 2 * half + 2, :, :]
-                if last_pass and half == 1:
+                if a == last and half == 1:
                     nc.scalar.copy(dst, src)
                 else:
                     nc.vector.tensor_copy(dst, src)
                 dealt.append(tile)
-            for half in range(2):
-                codes = keep.tile([P, 2 * P], U32, name="a_codes%d%d" % (a, half), align_bytes=64)
-                scales = keep.tile([P, 2 * P], U8, name="a_scales%d%d" % (a, half), align_bytes=64)
-                nc.vector.quantize_mx(out=codes[:].bitcast(FP8X4), scales=scales[:], in_=dealt[half][:].bitcast(BF16))
-                for tt in range(2):
-                    cols = slice(tt * P, (tt + 1) * P)
+            codes = keep.tile([P, J], U32, name="a_codes%d" % a, align_bytes=64)
+            scales = keep.tile([P, J], U8, name="a_scales%d" % a, align_bytes=64)
+            group = 1 if a == last else 2
+            for t0 in range(0, PACK, group):
+                cols = slice(t0 * P, (t0 + group) * P)
+                w0 = (t0 % 2) * 2 * P
+                nc.vector.quantize_mx(
+                    out=codes[:, cols].bitcast(FP8X4),
+                    scales=scales[:, cols],
+                    in_=dealt[t0 // 2][:, w0 : w0 + group * 2 * P].bitcast(BF16),
+                )
+                for t in range(t0, t0 + group):
+                    cols = slice(t * P, (t + 1) * P)
                     nc.tensor.matmul_mx(
-                        out=acc[2 * half + tt][:],
+                        out=acc[t][:],
                         lhsT=codes[:, cols].bitcast(FP8X4),
                         lhsT_scale=scales[:, cols],
                         rhs=picked_words[a][:].bitcast(FP4X4),
-                        rhs_scale=b_planes[a][:],
-                        start=(a == 0),
-                        stop=last_pass,
+                        rhs_scale=b_planes[:, a * I : (a + 1) * I],
+                        start=(a == first),
+                        stop=(a == last),
                     )
 
         y = keep.tile([P, PACK, I], F32, name="y")
         out_rows = out_0.rearrange("(p t) i -> t p i", t=PACK)
         cw_cols = cw_all[:].rearrange("p m n -> p n m")
+        relu, inv = [], []
         for t in range(PACK):
-            relu = keep.tile([P, I], F32, name="relu%d" % t)
-            total = keep.tile([P, 1], F32, name="total%d" % t)
+            relu.append(keep.tile([P, I], F32, name="relu%d" % t))
+            inv.append(keep.tile([P, 1], F32, name="inv%d" % t))
             denom = keep.tile([P, 1], F32, name="denom%d" % t)
-            inv = keep.tile([P, 1], F32, name="inv%d" % t)
-            nc.scalar.activation(relu[:], acc[t][:], ACT.Relu, accum_out=total[:])
-            nc.vector.tensor_scalar_add(denom[:], total[:], 1.0)
-            nc.vector.reciprocal(inv[:], denom[:])
-            nc.vector.scalar_tensor_tensor(
-                y[:, t, :].rearrange("p (n m) -> p n m", m=PACK),
-                relu[:].rearrange("p (n m) -> p n m", m=PACK),
-                inv[:],
-                cw_cols,
-                ALU.mult,
-                ALU.mult,
-            )
+            if t == 0:
+                nc.vector.tensor_scalar(relu[t][:], acc[t][:], 0.0, 1.0, ALU.max, ALU.add, accum_out=denom[:])
+            else:
+                total = keep.tile([P, 1], F32, name="total%d" % t)
+                nc.scalar.activation(relu[t][:], acc[t][:], ACT.Relu, accum_out=total[:])
+                nc.scalar.activation(denom[:], total[:], ACT.Copy, bias=1.0)
+            nc.vector.reciprocal(inv[t][:], denom[:])
+        for t in range(PACK):
+            width = HALF if t == PACK - 1 else I
+            for c0 in range(0, I, width):
+                nc.vector.scalar_tensor_tensor(
+                    y[:, t, c0 : c0 + width].rearrange("p (n m) -> p n m", m=PACK),
+                    relu[t][:, c0 : c0 + width].rearrange("p (n m) -> p n m", m=PACK),
+                    inv[t][:],
+                    cw_cols[:, c0 // PACK : (c0 + width) // PACK, :],
+                    ALU.mult,
+                    ALU.mult,
+                )
             nc.sync.dma_start(out_rows[t], y[:, t, :])
 
         y_bf = keep.tile([P, I, PACK], BF16, name="y_bf", align_bytes=64)
@@ -152,15 +177,21 @@ def tile_list_affinity_of_two_lists_pl_kernel(tc, xa, xb_words, xb_scales, cw1, 
         y_dst = y_bf[:].rearrange("p (c i) t -> p c t i", i=4)
         cut = OUT_SCALAR_COLS // 4
         nc.scalar.copy(y_dst[:, 0:cut], y_src[:, 0:cut])
-        nc.vector.tensor_copy(y_dst[:, cut:], y_src[:, cut:])
+        nc.vector.tensor_copy(y_dst[:, cut : HALF // 4], y_src[:, cut : HALF // 4])
+        nc.vector.tensor_copy(y_dst[:, HALF // 4 :], y_src[:, HALF // 4 :])
         y_codes = keep.tile([P, I], U32, name="y_codes", align_bytes=64)
         y_scales = keep.tile([P, I], U8, name="y_scales", align_bytes=64)
-        nc.vector.quantize_mx(
-            out=y_codes[:].bitcast(FP8X4), scales=y_scales[:], in_=y_bf[:].rearrange("p c t -> p (c t)")
-        )
-        nc.sync.dma_start(out_1[0].rearrange("p c r -> p (c r)").bitcast(I32), y_codes[:].bitcast(I32))
+        words_out = out_1[0].rearrange("p c r -> p (c r)").bitcast(I32)
+        for c0 in range(0, I, HALF):
+            cols = slice(c0, c0 + HALF)
+            nc.vector.quantize_mx(
+                out=y_codes[:, cols].bitcast(FP8X4),
+                scales=y_scales[:, cols],
+                in_=y_bf[:, cols, :].rearrange("p c t -> p (c t)"),
+            )
+            nc.sync.dma_start(words_out[:, cols], y_codes[:, cols].bitcast(I32))
         for q in range(4):
-            queue = nc.scalar if q % 2 else nc.sync
+            queue = nc.sync if q == 3 else nc.scalar
             queue.dma_start(
                 out_2[0, 4 * q : 4 * q + 4, :].bitcast(I32), y_scales[32 * q : 32 * q + 4, :].bitcast(I32)
             )

@@ -62,8 +62,8 @@ def tile_list_affinity_of_two_lists_pl_kernel(tc, xa, xb_words, xb_scales, cw1, 
         list_b = keep.tile([P, I // 16], U16, name="list_b")
         list_a = keep.tile([P, J // 16], U16, name="list_a")
         nc.sync.dma_start(list_b[:], offs2)
-        load_words(first)
         nc.sync.dma_start(b_scales[0:32, :].bitcast(I32), xb_scales.rearrange("z q c -> (z q) c").bitcast(I32))
+        load_words(first)
         for chunk in chunks[:2]:
             load_chunk(*chunk)
         load_words(last)
@@ -78,13 +78,13 @@ def tile_list_affinity_of_two_lists_pl_kernel(tc, xa, xb_words, xb_scales, cw1, 
             nc.vector.tensor_copy(picked[:], b_words[a][:].indirect(list_b[:]))
             picked_words[a] = picked
 
-        pick_words(first)
         picked_scales = keep.tile([P, I], U8, name="picked_scales", align_bytes=64)
         nc.vector.tensor_copy(picked_scales[:], b_scales[:].indirect(list_b[:]))
+        pick_words(first)
         pick_words(last)
         for a in PASS_ORDER:
-            queue = nc.gpsimd if a == first else nc.sync
             for q in range(4):
+                queue = nc.gpsimd if (a, q) == (first, 0) else nc.sync
                 queue.dma_start(
                     b_planes[32 * q : 32 * q + 4, a * I : (a + 1) * I].bitcast(I32),
                     picked_scales[16 * a + 4 * q : 16 * a + 4 * q + 4, :].bitcast(I32),

@@ -21,10 +21,10 @@ P = 128
 PACK = 4
 K_PASS = P * PACK
 PASS_ORDER = (0, 1)
-CHUNK = 512
+FIRST_SCALAR_COLS = 448
 HALF = I // 2
 LAST_SCALAR_COLS = 160
-OUT_SCALAR_COLS = 192
+OUT_SCALAR_COLS = 320
 
 
 def tile_list_affinity_of_two_lists_pl_kernel(tc, xa, xb_words, xb_scales, cw1, offs, offs2, out_0, out_1, out_2):
@@ -52,23 +52,23 @@ def tile_list_affinity_of_two_lists_pl_kernel(tc, xa, xb_words, xb_scales, cw1, 
             nc.sync.dma_start(words[:].bitcast(I32), xb_words[a].bitcast(I32))
             b_words[a] = words
 
-        def load_chunk(a, u, h):
+        def load_chunk(a, u, c0):
             rows = xa[a * K_PASS : (a + 1) * K_PASS, :].rearrange("(p u e) c -> u p e c", u=2, e=2)
-            chunk = keep.tile([P, 2, CHUNK], F32, name="raw%d%d%d" % (a, u, h))
-            nc.sync.dma_start(chunk[:], rows[u][:, :, h * CHUNK : (h + 1) * CHUNK])
-            raw[a, u, h] = chunk
+            chunk = keep.tile([P, 2, chunk_cols[a]], F32, name="raw%d%d_%d" % (a, u, c0))
+            nc.sync.dma_start(chunk[:], rows[u][:, :, c0 : c0 + chunk_cols[a]])
+            raw[a, u, c0] = chunk
 
-        chunks = [(a, u, h) for a in PASS_ORDER for u in range(2) for h in range(T // CHUNK)]
+        chunk_cols = {first: T, last: T // 2}
+        chunks = [(a, u, c0) for a in PASS_ORDER for u in range(2) for c0 in range(0, T, chunk_cols[a])]
         list_b = keep.tile([P, I // 16], U16, name="list_b")
         list_a = keep.tile([P, J // 16], U16, name="list_a")
         nc.sync.dma_start(list_b[:], offs2)
         nc.sync.dma_start(b_scales[0:32, :].bitcast(I32), xb_scales.rearrange("z q c -> (z q) c").bitcast(I32))
         load_words(first)
-        for chunk in chunks[:2]:
-            load_chunk(*chunk)
+        load_chunk(*chunks[0])
         load_words(last)
         nc.sync.dma_start(list_a[:], offs)
-        for chunk in chunks[2:]:
+        for chunk in chunks[1:]:
             load_chunk(*chunk)
 
         picked_words = {}
@@ -101,14 +101,18 @@ def tile_list_affinity_of_two_lists_pl_kernel(tc, xa, xb_words, xb_scales, cw1, 
             for u in range(2):
                 pairs = keep.tile([P, T], F32, name="pairs%d%d" % (a, u))
                 pairs_bf = pairs[:].bitcast(BF16).rearrange("p (c e) -> p c e", e=2)
-                for h in range(T // CHUNK):
-                    src = raw[a, u, h][:].rearrange("p e c -> p c e")
-                    c0 = h * CHUNK
-                    shared = h == T // CHUNK - 1 and u == 1
-                    cut = LAST_SCALAR_COLS if shared else CHUNK
+                width = chunk_cols[a]
+                for c0 in range(0, T, width):
+                    src = raw[a, u, c0][:].rearrange("p e c -> p c e")
+                    if a == first:
+                        cut = FIRST_SCALAR_COLS
+                    elif (a, u, c0) == chunks[-1]:
+                        cut = LAST_SCALAR_COLS
+                    else:
+                        cut = width
                     nc.scalar.activation(pairs_bf[:, c0 : c0 + cut, :], src[:, 0:cut, :], ACT.Copy)
-                    if cut < CHUNK:
-                        nc.vector.tensor_copy(pairs_bf[:, c0 + cut : c0 + CHUNK, :], src[:, cut:CHUNK, :])
+                    if cut < width:
+                        nc.vector.tensor_copy(pairs_bf[:, c0 + cut : c0 + width, :], src[:, cut:width, :])
                 nc.vector.tensor_copy(picked_a[:, u, :], pairs[:].indirect(list_a[:]))
             dealt_src = picked_a[:].rearrange("p u (mp mi t) -> p mp t mi u", mi=2, t=PACK)
             dealt = []
@@ -145,7 +149,7 @@ def tile_list_affinity_of_two_lists_pl_kernel(tc, xa, xb_words, xb_scales, cw1, 
                     )
 
         y = keep.tile([P, PACK, I], F32, name="y")
-        out_rows = out_0.rearrange("(p t) i -> t p i", t=PACK)
+        out_rows = out_0.rearrange("(p t) i -> p t i", t=PACK)
         cw_cols = cw_all[:].rearrange("p m n -> p n m")
         relu, inv = [], []
         for t in range(PACK):
@@ -159,26 +163,31 @@ def tile_list_affinity_of_two_lists_pl_kernel(tc, xa, xb_words, xb_scales, cw1, 
                 nc.scalar.activation(relu[t][:], acc[t][:], ACT.Relu, accum_out=total[:])
                 nc.scalar.activation(denom[:], total[:], ACT.Copy, bias=1.0)
             nc.vector.reciprocal(inv[t][:], denom[:])
-        for t in range(PACK):
-            width = HALF if t == PACK - 1 else I
-            for c0 in range(0, I, width):
-                nc.vector.scalar_tensor_tensor(
-                    y[:, t, c0 : c0 + width].rearrange("p (n m) -> p n m", m=PACK),
-                    relu[t][:, c0 : c0 + width].rearrange("p (n m) -> p n m", m=PACK),
-                    inv[t][:],
-                    cw_cols[:, c0 // PACK : (c0 + width) // PACK, :],
-                    ALU.mult,
-                    ALU.mult,
-                )
-            nc.sync.dma_start(out_rows[t], y[:, t, :])
+
+        def weigh(t, c0, width):
+            nc.vector.scalar_tensor_tensor(
+                y[:, t, c0 : c0 + width].rearrange("p (n m) -> p n m", m=PACK),
+                relu[t][:, c0 : c0 + width].rearrange("p (n m) -> p n m", m=PACK),
+                inv[t][:],
+                cw_cols[:, c0 // PACK : (c0 + width) // PACK, :],
+                ALU.mult,
+                ALU.mult,
+            )
+
+        weigh(0, 0, I)
+        nc.sync.dma_start(out_rows[:, 0, :], y[:, 0, :])
+        for c0 in range(0, I, HALF):
+            for t in range(1, PACK):
+                weigh(t, c0, HALF)
+            nc.sync.dma_start(out_rows[:, 1:PACK, c0 : c0 + HALF], y[:, 1:PACK, c0 : c0 + HALF])
 
         y_bf = keep.tile([P, I, PACK], BF16, name="y_bf", align_bytes=64)
         y_src = y[:].rearrange("p t (c i) -> p c t i", i=4)
         y_dst = y_bf[:].rearrange("p (c i) t -> p c t i", i=4)
         cut = OUT_SCALAR_COLS // 4
-        nc.scalar.copy(y_dst[:, 0:cut], y_src[:, 0:cut])
-        nc.vector.tensor_copy(y_dst[:, cut : HALF // 4], y_src[:, cut : HALF // 4])
-        nc.vector.tensor_copy(y_dst[:, HALF // 4 :], y_src[:, HALF // 4 :])
+        nc.scalar.copy(y_dst[:, 0 : HALF // 4], y_src[:, 0 : HALF // 4])
+        nc.scalar.copy(y_dst[:, HALF // 4 : cut], y_src[:, HALF // 4 : cut])
+        nc.vector.tensor_copy(y_dst[:, cut:], y_src[:, cut:])
         y_codes = keep.tile([P, I], U32, name="y_codes", align_bytes=64)
         y_scales = keep.tile([P, I], U8, name="y_scales", align_bytes=64)
         words_out = out_1[0].rearrange("p c r -> p (c r)").bitcast(I32)

from contextlib import ExitStack

import concourse.mybir as mybir
from concourse.masks import make_identity

K, T, S, J, I = 1024, 1024, 1024, 512, 512
FLOPS = 2 * K * J * I

F32 = mybir.dt.float32
BF16 = mybir.dt.bfloat16
I32 = mybir.dt.int32
U32 = mybir.dt.uint32
U16 = mybir.dt.uint16
U8 = mybir.dt.uint8
FP8X4 = mybir.dt.float8_e4m3fn_x4
FP4X4 = mybir.dt.float4_e2m1fn_x4
ACT = mybir.ActivationFunctionType
ALU = mybir.AluOpType

P = 128
PACK = 4
K_PASS = P * PACK
PASS_ORDER = (0, 1)
FIRST_SCALAR_COLS = 448
HALF = I // 2
LAST_SCALAR_COLS = 160
OUT_SCALAR_COLS = 320


def tile_list_affinity_of_two_lists_pl_kernel(tc, xa, xb_words, xb_scales, cw1, offs, offs2, out_0, out_1, out_2):
    nc = tc.nc
    first, last = PASS_ORDER
    with ExitStack() as ctx:
        keep = ctx.enter_context(tc.tile_pool(name="keep", bufs=1))
        psum = ctx.enter_context(tc.psum_pool(name="psum", bufs=1))

        b_scales = keep.tile([P, S], U8, name="b_scales")
        nc.gpsimd.memset(b_scales[32:64, :].bitcast(I32), 0)
        nc.gpsimd.memset(b_scales[64:P, :].bitcast(I32), 0)
        cw_col = keep.tile([P, PACK], F32, name="cw_col")
        nc.gpsimd.dma_start(cw_col[:], cw1.rearrange("o (n m) -> (o n) m", m=PACK))
        b_planes = keep.tile([P, 2 * I], U8, name="b_planes", align_bytes=64)
        nc.gpsimd.memset(b_planes[:].bitcast(I32), 0)
        ident = keep.tile([P, P], F32, name="ident")
        make_identity(nc, ident[:])

        raw = {}
        b_words = {}

        def load_words(a):
            words = keep.tile([P, S], U16, name="b_words%d" % a)
            nc.sync.dma_start(words[:].bitcast(I32), xb_words[a].bitcast(I32))
            b_words[a] = words

        def load_chunk(a, u, c0):
            rows = xa[a * K_PASS : (a + 1) * K_PASS, :].rearrange("(p u e) c -> u p e c", u=2, e=2)
            chunk = keep.tile([P, 2, chunk_cols[a]], F32, name="raw%d%d_%d" % (a, u, c0))
            nc.sync.dma_start(chunk[:], rows[u][:, :, c0 : c0 + chunk_cols[a]])
            raw[a, u, c0] = chunk

        chunk_cols = {first: T, last: T // 2}
        chunks = [(a, u, c0) for a in PASS_ORDER for u in range(2) for c0 in range(0, T, chunk_cols[a])]
        list_b = keep.tile([P, I // 16], U16, name="list_b")
        list_a = keep.tile([P, J // 16], U16, name="list_a")
        nc.sync.dma_start(list_b[:], offs2)
        nc.sync.dma_start(b_scales[0:32, :].bitcast(I32), xb_scales.rearrange("z q c -> (z q) c").bitcast(I32))
        load_words(first)
        load_chunk(*chunks[0])
        load_words(last)
        nc.sync.dma_start(list_a[:], offs)
        for chunk in chunks[1:]:
            load_chunk(*chunk)

        picked_words = {}

        def pick_words(a):
            picked = keep.tile([P, I], U16, name="picked_words%d" % a, align_bytes=64)
            nc.vector.tensor_copy(picked[:], b_words[a][:].indirect(list_b[:]))
            picked_words[a] = picked

        picked_scales = keep.tile([P, I], U8, name="picked_scales", align_bytes=64)
        nc.vector.tensor_copy(picked_scales[:], b_scales[:].indirect(list_b[:]))
        pick_words(first)
        pick_words(last)
        for a in PASS_ORDER:
            for q in range(4):
                queue = nc.gpsimd if (a, q) == (first, 0) else nc.sync
                queue.dma_start(
                    b_planes[32 * q : 32 * q + 4, a * I : (a + 1) * I].bitcast(I32),
                    picked_scales[16 * a + 4 * q : 16 * a + 4 * q + 4, :].bitcast(I32),
                )

        cw_all = psum.tile([P, PACK, P], F32, name="cw_all")
        for m in range(PACK):
            nc.tensor.transpose(cw_all[:, m, :], cw_col[:, m : m + 1].to_broadcast([P, P]), ident[:])

        acc = [psum.tile([P, I], F32, name="acc%d" % t) for t in range(PACK)]

        for a in PASS_ORDER:
            picked_a = keep.tile([P, 2, J], F32, name="picked_a%d" % a)
            for u in range(2):
                pairs = keep.tile([P, T], F32, name="pairs%d%d" % (a, u))
                pairs_bf = pairs[:].bitcast(BF16).rearrange("p (c e) -> p c e", e=2)
                width = chunk_cols[a]
                for c0 in range(0, T, width):
                    src = raw[a, u, c0][:].rearrange("p e c -> p c e")
                    if a == first:
                        cut = FIRST_SCALAR_COLS
                    elif (a, u, c0) == chunks[-1]:
                        cut = LAST_SCALAR_COLS
                    else:
                        cut = width
                    nc.scalar.activation(pairs_bf[:, c0 : c0 + cut, :], src[:, 0:cut, :], ACT.Copy)
                    if cut < width:
                        nc.vector.tensor_copy(pairs_bf[:, c0 + cut : c0 + width, :], src[:, cut:width, :])
                nc.vector.tensor_copy(picked_a[:, u, :], pairs[:].indirect(list_a[:]))
            dealt_src = picked_a[:].rearrange("p u (mp mi t) -> p mp t mi u", mi=2, t=PACK)
            dealt = []
            for half in range(2):
                tile = keep.tile([P, 2 * P * 2], F32, name="dealt%d%d" % (a, half), align_bytes=64)
                dst = tile[:].rearrange("p (t mp mi u) -> p mp t mi u", t=2, mi=2, u=2)
                src = dealt_src[:, :, 2 * half : 2 * half + 2, :, :]
                if a == last and half == 1:
                    nc.scalar.copy(dst, src)
                else:
                    nc.vector.tensor_copy(dst, src)
                dealt.append(tile)
            codes = keep.tile([P, J], U32, name="a_codes%d" % a, align_bytes=64)
            scales = keep.tile([P, J], U8, name="a_scales%d" % a, align_bytes=64)
            group = 1 if a == last else 2
            for t0 in range(0, PACK, group):
                cols = slice(t0 * P, (t0 + group) * P)
                w0 = (t0 % 2) * 2 * P
                nc.vector.quantize_mx(
                    out=codes[:, cols].bitcast(FP8X4),
                    scales=scales[:, cols],
                    in_=dealt[t0 // 2][:, w0 : w0 + group * 2 * P].bitcast(BF16),
                )
                for t in range(t0, t0 + group):
                    cols = slice(t * P, (t + 1) * P)
                    nc.tensor.matmul_mx(
                        out=acc[t][:],
                        lhsT=codes[:, cols].bitcast(FP8X4),
                        lhsT_scale=scales[:, cols],
                        rhs=picked_words[a][:].bitcast(FP4X4),
                        rhs_scale=b_planes[:, a * I : (a + 1) * I],
                        start=(a == first),
                        stop=(a == last),
                    )

        y = keep.tile([P, PACK, I], F32, name="y")
        out_rows = out_0.rearrange("(p t) i -> p t i", t=PACK)
        cw_cols = cw_all[:].rearrange("p m n -> p n m")
        relu, inv = [], []
        for t in range(PACK):
            relu.append(keep.tile([P, I], F32, name="relu%d" % t))
            inv.append(keep.tile([P, 1], F32, name="inv%d" % t))
            denom = keep.tile([P, 1], F32, name="denom%d" % t)
            if t == 0:
                nc.vector.tensor_scalar(relu[t][:], acc[t][:], 0.0, 1.0, ALU.max, ALU.add, accum_out=denom[:])
            else:
                total = keep.tile([P, 1], F32, name="total%d" % t)
                nc.scalar.activation(relu[t][:], acc[t][:], ACT.Relu, accum_out=total[:])
                nc.scalar.activation(denom[:], total[:], ACT.Copy, bias=1.0)
            nc.vector.reciprocal(inv[t][:], denom[:])

        def weigh(t, c0, width):
            nc.vector.scalar_tensor_tensor(
                y[:, t, c0 : c0 + width].rearrange("p (n m) -> p n m", m=PACK),
                relu[t][:, c0 : c0 + width].rearrange("p (n m) -> p n m", m=PACK),
                inv[t][:],
                cw_cols[:, c0 // PACK : (c0 + width) // PACK, :],
                ALU.mult,
                ALU.mult,
            )

        weigh(0, 0, I)
        nc.sync.dma_start(out_rows[:, 0, :], y[:, 0, :])
        for c0 in range(0, I, HALF):
            for t in range(1, PACK):
                weigh(t, c0, HALF)
            nc.sync.dma_start(out_rows[:, 1:PACK, c0 : c0 + HALF], y[:, 1:PACK, c0 : c0 + HALF])

        y_bf = keep.tile([P, I, PACK], BF16, name="y_bf", align_bytes=64)
        y_src = y[:].rearrange("p t (c i) -> p c t i", i=4)
        y_dst = y_bf[:].rearrange("p (c i) t -> p c t i", i=4)
        cut = OUT_SCALAR_COLS // 4
        nc.scalar.copy(y_dst[:, 0 : HALF // 4], y_src[:, 0 : HALF // 4])
        nc.scalar.copy(y_dst[:, HALF // 4 : cut], y_src[:, HALF // 4 : cut])
        nc.vector.tensor_copy(y_dst[:, cut:], y_src[:, cut:])
        y_codes = keep.tile([P, I], U32, name="y_codes", align_bytes=64)
        y_scales = keep.tile([P, I], U8, name="y_scales", align_bytes=64)
        words_out = out_1[0].rearrange("p c r -> p (c r)").bitcast(I32)
        for c0 in range(0, I, HALF):
            cols = slice(c0, c0 + HALF)
            nc.vector.quantize_mx(
                out=y_codes[:, cols].bitcast(FP8X4),
                scales=y_scales[:, cols],
                in_=y_bf[:, cols, :].rearrange("p c t -> p (c t)"),
            )
            nc.sync.dma_start(words_out[:, cols], y_codes[:, cols].bitcast(I32))
        for q in range(4):
            queue = nc.sync if q == 3 else nc.scalar
            queue.dma_start(
                out_2[0, 4 * q : 4 * q + 4, :].bitcast(I32), y_scales[32 * q : 32 * q + 4, :].bitcast(I32)
            )
